import numpy as np
import ml_dtypes


def mxq(x, axis, fmt="e4m3"):
    dtype, down = {"e4m3": (ml_dtypes.float8_e4m3fn, 7), "e5m2": (ml_dtypes.float8_e5m2, 14)}[fmt]
    v = np.moveaxis(np.asarray(x, np.float32).astype(ml_dtypes.bfloat16).astype(np.float64), axis, -1)
    blocks = v.reshape(v.shape[:-1] + (-1, 32))
    amax = np.abs(blocks).max(-1, keepdims=True)
    byte = np.maximum(np.where(amax > 0, np.frexp(amax)[1] - 1 + 127, 0) - down, 1)
    scale = np.exp2(byte - 127.0)
    codes = (blocks / scale).astype(np.float32).astype(dtype).astype(np.float64)
    return np.moveaxis((codes * scale).reshape(v.shape), -1, axis)


WIDE = False


def mx_kscale(k):
    if not WIDE:
        return np.ones(k)
    levels = np.array([10, -10, 5, -5, 0])
    if k % 512:
        return np.exp2(np.random.permutation(np.resize(levels, k // 32))).repeat(32)
    a = np.empty((k // 512, 16))
    for p in range(k // 512):
        a[p, :8] = np.random.permutation(np.resize(levels, 8))
        for g in range(8):
            far = levels[np.abs(levels - a[p, g]) >= 10]
            a[p, g + 8] = far[np.random.randint(len(far))]
    return np.exp2(a.ravel()).repeat(32)


BF16 = ml_dtypes.bfloat16


def bf(x):
    return np.asarray(x, np.float32).astype(BF16)


def f64(x):
    return np.asarray(x).astype(np.float64)


E2M1 = np.array([0.0, 0.5, 1.0, 1.5, 2.0, 3.0, 4.0, 6.0, -0.0, -0.5, -1.0, -1.5, -2.0, -3.0, -4.0, -6.0])


def pack_weight(w, fmt):
    k, n = w.shape
    w = f64(bf(w)).reshape(k // 32, 32, n)
    amax = np.abs(w).max(1)
    if fmt == "e4m3":
        byte = np.frexp(amax)[1] - 1 + 127 - 7
    else:
        mant, ex = np.frexp(amax / 6.0)
        byte = np.where(mant > 0.5, ex, ex - 1) + 127
    byte = np.clip(np.where(amax > 0, byte, 1), 1, 254)
    scaled = (w * np.exp2(127.0 - byte)[:, None, :]).reshape(k, n).astype(np.float32)
    by_word = np.ascontiguousarray(scaled.reshape(k // 512, 128, 4, n).transpose(0, 1, 3, 2))
    if fmt == "e4m3":
        words = by_word.astype(ml_dtypes.float8_e4m3fn).view(np.uint8)
    else:
        c = by_word.astype(ml_dtypes.float4_e2m1fn).view(np.uint8) & 0xF
        words = c[..., 0::2] | (c[..., 1::2] << 4)
    return np.ascontiguousarray(words), np.ascontiguousarray(byte.astype(np.uint8).reshape(k // 512, 16, n))


def unpack_weight(words, scales, fmt):
    g, p, n, _ = words.shape
    if fmt == "e4m3":
        vals = np.ascontiguousarray(words).view(ml_dtypes.float8_e4m3fn).astype(np.float64)
    else:
        nib = np.empty((g, p, n, 4), np.uint8)
        nib[..., 0::2] = words & 0xF
        nib[..., 1::2] = words >> 4
        vals = E2M1[nib]
    vals = vals * np.repeat(np.exp2(scales.astype(np.float64) - 127.0), 8, axis=1)[..., None]
    return vals.transpose(0, 1, 3, 2).reshape(g * 512, n)
def pack4(w):
    words, scales = pack_weight(w, "e2m1")
    return words.reshape(words.shape[0], 128, -1), scales


def unpack4(words, scales):
    return unpack_weight(words.reshape(words.shape[0], 128, -1, 2), scales, "e2m1")


D, B, Q = 1024, 1024, 2048


def setup_inputs():
    s, u = mx_kscale(B), mx_kscale(Q)
    za = np.random.standard_normal((B, D)) * s[:, None]
    zb = np.random.standard_normal((B, D)) / np.sqrt(B + Q) / s[:, None]
    ma = np.random.standard_normal((D, Q)) * u
    mb = np.random.standard_normal((Q, D)) / np.sqrt(B + Q) / u[:, None]
    mb_words, mb_scales = pack4(mb)
    return {"za": bf(za),
            "zb": bf(zb),
            "ma": bf(ma),
            "mb_words": mb_words,
            "mb_scales": mb_scales,
            "ra": bf(1 + 0.1 * np.random.standard_normal(D)),
            "rb": bf(1 + 0.1 * np.random.standard_normal(D)),
            "goal": bf(8 + 0.8 * np.random.standard_normal(D)),
            "pair": bf(0.6 + 0.1 * np.random.standard_normal((D, D)) + 0.4 * np.eye(D))}


def reference(za, zb, ma, mb_words, mb_scales, ra, rb, goal, pair):
    live = mxq(f64(za), 0, "e4m3").T @ mxq(f64(zb), 0, "e4m3")
    bank = mxq(f64(ma), 1, "e4m3") @ unpack4(mb_words, mb_scales)
    c = (live + bank) * f64(ra)[:, None] * f64(rb)[None, :]
    return f64(pair) * (c - np.eye(D) * f64(goal)[None, :])

@@ -1,0 +1,354 @@
+from contextlib import ExitStack
+
+import concourse.mybir as mybir
+from concourse.masks import make_identity
+
+F32 = mybir.dt.float32
+BF16 = mybir.dt.bfloat16
+U32 = mybir.dt.uint32
+I32 = mybir.dt.int32
+U8 = mybir.dt.uint8
+FP8X4 = mybir.dt.float8_e4m3fn_x4
+FP4X4 = mybir.dt.float4_e2m1fn_x4
+MULT = mybir.AluOpType.mult
+ADD = mybir.AluOpType.add
+SUB = mybir.AluOpType.subtract
+
+D, B, Q = 1024, 1024, 2048
+P = 128
+N = 512
+KP = 512
+FLOPS = 2 * D * D * (B + Q)
+V_COLS = 336
+
+
+def tile_barlow_twins_bank_s1_kernel(tc, za, zb, ma, mb_words, mb_scales, ra, rb, goal, pair, out):
+    nc = tc.nc
+    with ExitStack() as ctx:
+        keep = ctx.enter_context(tc.tile_pool(name="keep", bufs=1))
+        stage = ctx.enter_context(tc.tile_pool(name="stage", bufs=4))
+        psum = ctx.enter_context(tc.psum_pool(name="psum", bufs=1))
+        ctx.enter_context(tc.manual_schedule())
+
+        ident = keep.tile([P, P], F32, name="ident", align_bytes=64)
+        ident_bf = keep.tile([P, P], BF16, name="ident_bf", align_bytes=64)
+        vec = keep.tile([P, P], BF16, name="vec", align_bytes=64)
+        cols = keep.tile([P, 24], F32, name="cols", align_bytes=64)
+        rb_col = keep.tile([P, 8], BF16, name="rb_col", align_bytes=64)
+        rb_all = keep.tile([P, D], BF16, name="rb_all", align_bytes=64)
+        goal_diag = keep.tile([P, 8, P], F32, name="goal_diag", align_bytes=64)
+        mbw = keep.tile([P, 4, 2 * D], U8, name="mbw", align_bytes=64)
+        mbs = keep.tile([P, 4, D], U8, name="mbs", align_bytes=64)
+        za_codes = keep.tile([P, 2, D], U32, name="za_codes", align_bytes=64)
+        za_scales = keep.tile([P, 2, D], U8, name="za_scales", align_bytes=64)
+        zb_codes = keep.tile([P, 2, D], U32, name="zb_codes", align_bytes=64)
+        zb_scales = keep.tile([P, 2, D], U8, name="zb_scales", align_bytes=64)
+        ma_codes = [keep.tile([P, 4, P], U32, name="ma_codes%d" % i, align_bytes=64) for i in range(8)]
+        ma_scales = [keep.tile([P, 4, P], U8, name="ma_scales%d" % i, align_bytes=64) for i in range(8)]
+        ma_raw = [keep.tile([P, Q], BF16, name="ma_raw%d" % i, align_bytes=64) for i in range(8)]
+        zb_raw = [keep.tile([P, 4, D], BF16, name="zb_raw%d" % g, align_bytes=64) for g in range(2)]
+        za_raw = [[keep.tile([P, 4, N], BF16, name="za_raw%d%d" % (g, h), align_bytes=64) for h in range(2)] for g in range(2)]
+        pair_sb = [keep.tile([P, 2, D], BF16, name="pair%d" % i, align_bytes=64) for i in range(4)]
+
+        za_v = za.rearrange("(g p j) w -> g p j w", p=P, j=4)
+        zb_v = zb.rearrange("(g p j) w -> g p j w", p=P, j=4)
+        pair_v = pair.rearrange("(a i p) n -> a p i n", i=2, p=P)
+        mbw_v = mb_words.bitcast(I32).rearrange("g p b -> p g b")
+
+        def load_ma(i, k0=0, k1=Q):
+            nc.sync.dma_start(out=ma_raw[i][:, k0:k1], in_=ma[P * i : P * (i + 1), k0:k1])
+
+        def load_mb(a):
+            nc.sync.dma_start(out=mbw[:, 2 * a : 2 * a + 2, :].bitcast(I32), in_=mbw_v[:, 2 * a : 2 * a + 2, :])
+
+        def load_zb(g):
+            nc.sync.dma_start(out=zb_raw[g][:], in_=zb_v[g])
+
+        def load_za(g, h):
+            nc.sync.dma_start(out=za_raw[g][h][:], in_=za_v[g][:, :, N * h : N * (h + 1)])
+
+        def load_pair(a):
+            nc.sync.dma_start(out=pair_sb[a][:], in_=pair_v[a])
+
+        nc.vector.memset(mbs[:].rearrange("p g n -> p (g n)").bitcast(I32), 0)
+        nc.vector.memset(vec[:], 0.0)
+        for q in range(4):
+            nc.scalar.dma_start(
+                out=mbs[32 * q : 32 * q + 4, :, :].bitcast(I32),
+                in_=mb_scales[:, 4 * q : 4 * q + 4, :].bitcast(I32).rearrange("g r n -> r g n"),
+            )
+        make_identity(nc, ident[:])
+        for v, src in enumerate((ra, rb, goal)):
+            nc.gpsimd.dma_start(out=vec[8 * v : 8 * v + 8, :], in_=src.rearrange("(c p) -> c p", p=P))
+        nc.vector.tensor_copy(out=ident_bf[:], in_=ident[:])
+
+        load_ma(0, 0, D)
+        load_ma(0, D, Q)
+        load_mb(0)
+        load_ma(1)
+        load_mb(1)
+        load_ma(2)
+        load_ma(3)
+        load_zb(0)
+        load_ma(4)
+        load_za(0, 0)
+        load_zb(1)
+        load_za(1, 0)
+        load_pair(0)
+        load_pair(1)
+        load_za(0, 1)
+        load_ma(5)
+        load_za(1, 1)
+        load_ma(6)
+        load_pair(2)
+        load_ma(7)
+        load_pair(3)
+
+        turned = {}
+        grouped = {}
+        zgrouped = {}
+        acc = {}
+        weight = {}
+        result = {}
+        diag = {}
+
+        def T(i, b, bank):
+            t = psum.tile([P, 2, 2, P], F32, name="turned%d_%d" % (i, b), tag="bank%d" % bank)
+            turned[i, b] = t
+            words = ma_raw[i][:].bitcast(F32)
+            for gg in range(2):
+                g = 2 * b + gg
+                for u in range(2):
+                    nc.tensor.transpose(t[:, gg, u, :], words[:, 256 * g + u : 256 * (g + 1) : 2], ident[:])
+
+        def C(eng, i, b):
+            if i not in grouped:
+                grouped[i] = stage.tile([P, 4, P, 4], BF16, name="ma_grouped%d" % i, tag="ma_grouped", align_bytes=64)
+            dst = grouped[i][:, 2 * b : 2 * b + 2, :, :].rearrange("p g m t -> p (g m t)").bitcast(F32)
+            dst = dst.rearrange("p (g m u) -> p g m u", g=2, u=2)
+            src = turned[i, b][:].rearrange("p g u m -> p g m u")
+            if eng == "S":
+                nc.scalar.copy(out=dst, in_=src)
+            else:
+                nc.vector.tensor_copy(out=dst, in_=src)
+
+        def QM(i, g0=0, g1=4):
+            nc.vector.quantize_mx(
+                out=ma_codes[i][:, g0:g1, :].rearrange("p g m -> p (g m)").bitcast(FP8X4),
+                scales=ma_scales[i][:, g0:g1, :].rearrange("p g m -> p (g m)"),
+                in_=grouped[i][:, g0:g1, :, :].rearrange("p g m t -> p (g m t)"),
+            )
+
+        def I(eng, z, g, h, v_cols=V_COLS):
+            if (z, g, h) not in zgrouped:
+                zgrouped[z, g, h] = stage.tile([P, N, 4], BF16, name="%s_grouped%d%d" % (z, g, h), tag="z_grouped", align_bytes=64)
+            dst = zgrouped[z, g, h]
+            src = zb_raw[g][:, :, N * h : N * (h + 1)] if z == "zb" else za_raw[g][h][:]
+            if eng == "V":
+                nc.vector.tensor_copy(out=dst[:, 0:v_cols, :], in_=src[:, :, 0:v_cols].rearrange("p j w -> p w j"))
+            else:
+                nc.scalar.copy(out=dst[:, v_cols:N, :], in_=src[:, :, v_cols:N].rearrange("p j w -> p w j"))
+
+        def Z(z, g, h):
+            codes, scales = (zb_codes, zb_scales) if z == "zb" else (za_codes, za_scales)
+            nc.vector.quantize_mx(
+                out=codes[:, g, N * h : N * (h + 1)].bitcast(FP8X4),
+                scales=scales[:, g, N * h : N * (h + 1)],
+                in_=zgrouped[z, g, h][:].rearrange("p w j -> p (w j)"),
+            )
+
+        def bank_pass(i, h, gs, bank):
+            if (i, h) not in acc:
+                acc[i, h] = psum.tile([P, N], F32, name="acc%d_%d" % (i, h), tag="bank%d" % bank)
+            for g in gs:
+                nc.tensor.matmul_mx(
+                    out=acc[i, h][:],
+                    lhsT=ma_codes[i][:, g, :].bitcast(FP8X4),
+                    lhsT_scale=ma_scales[i][:, g, :],
+                    rhs=mbw[:, g, 2 * N * h : 2 * N * (h + 1)].bitcast(FP4X4),
+                    rhs_scale=mbs[:, g, N * h : N * (h + 1)],
+                    start=(g == 0),
+                    stop=False,
+                )
+
+        def L(i, h, g):
+            nc.tensor.matmul_mx(
+                out=acc[i, h][:],
+                lhsT=za_codes[:, g, P * i : P * (i + 1)].bitcast(FP8X4),
+                lhsT_scale=za_scales[:, g, P * i : P * (i + 1)],
+                rhs=zb_codes[:, g, N * h : N * (h + 1)].bitcast(FP8X4),
+                rhs_scale=zb_scales[:, g, N * h : N * (h + 1)],
+                start=False,
+                stop=(g == 1),
+            )
+
+        def W(eng, i):
+            w = stage.tile([P, D], F32, name="weight%d" % i, tag="weight", bufs=6, align_bytes=64)
+            weight[i] = w
+            src = pair_sb[i // 2][:, i % 2, :]
+            if eng == "G":
+                for h in range(2):
+                    c = slice(N * h, N * (h + 1))
+                    nc.gpsimd.tensor_tensor(out=w[:, c], in0=src[:, c], in1=rb_all[:, c], op=MULT)
+            else:
+                nc.vector.tensor_tensor(out=w[:], in0=src, in1=rb_all[:], op=MULT)
+            d = stage.tile([P, P], F32, name="diag%d" % i, tag="diag", align_bytes=64)
+            diag[i] = d
+            nc.gpsimd.tensor_tensor(out=d[:], in0=src[:, P * i : P * (i + 1)], in1=goal_diag[:, i, :], op=MULT)
+
+        def E(i, h):
+            if i not in result:
+                result[i] = stage.tile([P, D], F32, name="result%d" % i, tag="result", bufs=6, align_bytes=64)
+            c = slice(N * h, N * (h + 1))
+            nc.vector.scalar_tensor_tensor(
+                out=result[i][:, c], in0=acc[i, h][:], scalar=cols[:, i : i + 1], in1=weight[i][:, c], op0=MULT, op1=MULT
+            )
+            if h == i // 4:
+                blk = result[i][:, P * i : P * (i + 1)]
+                nc.gpsimd.tensor_tensor(out=blk, in0=blk, in1=diag[i][:], op=SUB)
+
+        def store(i, h=None):
+            c = slice(0, D) if h is None else slice(N * h, N * (h + 1))
+            nc.sync.dma_start(out=out[P * i : P * (i + 1), c], in_=result[i][:, c])
+
+        def vectors():
+            t = psum.tile([P, P], BF16, name="vec_t", tag="bank6")
+            nc.tensor.transpose(t[:], vec[:], ident_bf[:])
+            nc.vector.tensor_copy(out=rb_col[:], in_=t[:, 8:16])
+            nc.vector.tensor_copy(out=cols[:], in_=t[:, 0:24])
+
+        def spread_rb():
+            t = psum.tile([P, D], BF16, name="rb_t", tag="bank7")
+            for c in range(8):
+                nc.tensor.transpose(t[:, P * c : P * (c + 1)], rb_col[:, c : c + 1].to_broadcast([P, P]), ident_bf[:])
+            nc.scalar.copy(out=rb_all[:], in_=t[:])
+            for i in range(8):
+                nc.gpsimd.tensor_scalar(out=goal_diag[:, i, :], in0=ident[:], scalar1=cols[:, 16 + i : 17 + i], scalar2=0.0, op0=MULT, op1=ADD)
+
+        def halves(i):
+            return (1, 0) if i >= 4 else (0, 1)
+
+        def both_T(i, bank):
+            T(i, 0, bank)
+            T(i, 1, bank + 1)
+
+        def bank_product(i, bank, gs=(0, 1, 2, 3)):
+            for h in halves(i):
+                bank_pass(i, h, gs, bank + h)
+
+        both_T(0, 0)
+        C("S", 0, 0)
+        C("V", 0, 1)
+        QM(0, 0, 2)
+        QM(0, 2, 4)
+        bank_product(0, 4, (0, 1))
+        both_T(1, 2)
+        C("S", 1, 0)
+        C("V", 1, 1)
+        vectors()
+        bank_product(0, 4, (2, 3))
+        QM(1)
+        spread_rb()
+        both_T(2, 0)
+        C("S", 2, 0)
+        C("V", 2, 1)
+        both_T(3, 2)
+        C("S", 3, 0)
+        QM(2)
+        C("V", 3, 1)
+        bank_product(1, 6)
+        I("S", "zb", 0, 0)
+        I("V", "zb", 0, 0)
+        I("S", "zb", 0, 1)
+        QM(3)
+        I("V", "zb", 0, 1)
+        both_T(4, 0)
+        C("S", 4, 0)
+        C("S", 4, 1)
+        Z("zb", 0, 0)
+        bank_product(2, 2)
+        I("V", "za", 0, 0)
+        I("S", "za", 0, 0)
+        Z("zb", 0, 1)
+        Z("za", 0, 0)
+        for i in range(3):
+            L(i, 0, 0)
+            L(i, 1, 0)
+        I("S", "zb", 1, 0)
+        I("V", "zb", 1, 0)
+        I("S", "zb", 1, 1)
+        I("V", "zb", 1, 1)
+        Z("zb", 1, 0)
+        bank_product(3, 0)
+        W("G", 0)
+        I("S", "za", 1, 0)
+        I("V", "za", 1, 0)
+        Z("zb", 1, 1)
+        Z("za", 1, 0)
+        L(3, 0, 0)
+        L(3, 1, 0)
+        QM(4)
+        W("G", 1)
+        I("S", "za", 0, 1, 0)
+        for i in range(4):
+            L(i, 0, 1)
+            L(i, 1, 1)
+        E(0, 0)
+        E(0, 1)
+        store(0)
+        W("G", 2)
+        I("S", "za", 1, 1, 0)
+        E(1, 0)
+        E(1, 1)
+        store(1)
+        both_T(5, 4)
+        C("S", 5, 0)
+        C("S", 5, 1)
+        Z("za", 0, 1)
+        bank_product(4, 6)
+        W("G", 3)
+        E(2, 0)
+        E(2, 1)
+        store(2)
+        Z("za", 1, 1)
+        QM(5)
+        W("G", 4)
+        both_T(6, 2)
+        C("S", 6, 0)
+        C("S", 6, 1)
+        E(3, 0)
+        E(3, 1)
+        store(3)
+        for h in halves(4):
+            L(4, h, 0)
+            L(4, h, 1)
+        W("V", 6)
+        QM(6)
+        W("G", 5)
+        bank_product(5, 0)
+        for h in halves(4):
+            E(4, h)
+        store(4)
+        for h in halves(5):
+            L(5, h, 0)
+            L(5, h, 1)
+        W("V", 7)
+        both_T(7, 4)
+        C("S", 7, 0)
+        C("S", 7, 1)
+        for h in halves(5):
+            E(5, h)
+        store(5)
+        QM(7)
+        bank_product(6, 6)
+        for h in halves(6):
+            L(6, h, 0)
+            L(6, h, 1)
+            E(6, h)
+        store(6)
+        bank_product(7, 2)
+        for h in halves(7):
+            L(7, h, 0)
+            L(7, h, 1)
+            E(7, h)
+            store(7, h)

@@ -11,7 +11,6 @@ U8 = mybir.dt.uint8
 FP8X4 = mybir.dt.float8_e4m3fn_x4
 FP4X4 = mybir.dt.float4_e2m1fn_x4
 MULT = mybir.AluOpType.mult
-ADD = mybir.AluOpType.add
 SUB = mybir.AluOpType.subtract
 
 D, B, Q = 1024, 1024, 2048
@@ -19,7 +18,7 @@ P = 128
 N = 512
 KP = 512
 FLOPS = 2 * D * D * (B + Q)
-V_COLS = 336
+V_COLS = 192
 
 
 def tile_barlow_twins_bank_s1_kernel(tc, za, zb, ma, mb_words, mb_scales, ra, rb, goal, pair, out):
@@ -78,14 +77,14 @@ def tile_barlow_twins_bank_s1_kernel(tc, za, zb, ma, mb_words, mb_scales, ra, rb
                 in_=mb_scales[:, 4 * q : 4 * q + 4, :].bitcast(I32).rearrange("g r n -> r g n"),
             )
         make_identity(nc, ident[:])
-        for v, src in enumerate((ra, rb, goal)):
-            nc.gpsimd.dma_start(out=vec[8 * v : 8 * v + 8, :], in_=src.rearrange("(c p) -> c p", p=P))
         nc.vector.tensor_copy(out=ident_bf[:], in_=ident[:])
 
         load_ma(0, 0, D)
         load_ma(0, D, Q)
         load_mb(0)
         load_ma(1)
+        for v, src in enumerate((ra, rb, goal)):
+            nc.scalar.dma_start(out=vec[8 * v : 8 * v + 8, :], in_=src.rearrange("(c p) -> c p", p=P))
         load_mb(1)
         load_ma(2)
         load_ma(3)
@@ -182,16 +181,11 @@ def tile_barlow_twins_bank_s1_kernel(tc, za, zb, ma, mb_words, mb_scales, ra, rb
                 stop=(g == 1),
             )
 
-        def W(eng, i):
+        def W(i):
             w = stage.tile([P, D], F32, name="weight%d" % i, tag="weight", bufs=6, align_bytes=64)
             weight[i] = w
             src = pair_sb[i // 2][:, i % 2, :]
-            if eng == "G":
-                for h in range(2):
-                    c = slice(N * h, N * (h + 1))
-                    nc.gpsimd.tensor_tensor(out=w[:, c], in0=src[:, c], in1=rb_all[:, c], op=MULT)
-            else:
-                nc.vector.tensor_tensor(out=w[:], in0=src, in1=rb_all[:], op=MULT)
+            nc.vector.tensor_tensor(out=w[:], in0=src, in1=rb_all[:], op=MULT)
             d = stage.tile([P, P], F32, name="diag%d" % i, tag="diag", align_bytes=64)
             diag[i] = d
             nc.gpsimd.tensor_tensor(out=d[:], in0=src[:, P * i : P * (i + 1)], in1=goal_diag[:, i, :], op=MULT)
@@ -216,14 +210,18 @@ def tile_barlow_twins_bank_s1_kernel(tc, za, zb, ma, mb_words, mb_scales, ra, rb
             nc.tensor.transpose(t[:], vec[:], ident_bf[:])
             nc.vector.tensor_copy(out=rb_col[:], in_=t[:, 8:16])
             nc.vector.tensor_copy(out=cols[:], in_=t[:, 0:24])
+            nc.vector.tensor_tensor(
+                out=goal_diag[:],
+                in0=ident[:].unsqueeze(1).to_broadcast([P, 8, P]),
+                in1=cols[:, 16:24].unsqueeze(2).to_broadcast([P, 8, P]),
+                op=MULT,
+            )
 
         def spread_rb():
             t = psum.tile([P, D], BF16, name="rb_t", tag="bank7")
             for c in range(8):
                 nc.tensor.transpose(t[:, P * c : P * (c + 1)], rb_col[:, c : c + 1].to_broadcast([P, P]), ident_bf[:])
             nc.scalar.copy(out=rb_all[:], in_=t[:])
-            for i in range(8):
-                nc.gpsimd.tensor_scalar(out=goal_diag[:, i, :], in0=ident[:], scalar1=cols[:, 16 + i : 17 + i], scalar2=0.0, op0=MULT, op1=ADD)
 
         def halves(i):
             return (1, 0) if i >= 4 else (0, 1)
@@ -245,11 +243,11 @@ def tile_barlow_twins_bank_s1_kernel(tc, za, zb, ma, mb_words, mb_scales, ra, rb
         both_T(1, 2)
         C("S", 1, 0)
         C("V", 1, 1)
-        vectors()
         bank_product(0, 4, (2, 3))
         QM(1)
-        spread_rb()
+        vectors()
         both_T(2, 0)
+        spread_rb()
         C("S", 2, 0)
         C("V", 2, 1)
         both_T(3, 2)
@@ -259,36 +257,37 @@ def tile_barlow_twins_bank_s1_kernel(tc, za, zb, ma, mb_words, mb_scales, ra, rb
         bank_product(1, 6)
         I("S", "zb", 0, 0)
         I("V", "zb", 0, 0)
-        I("S", "zb", 0, 1)
         QM(3)
+        I("S", "zb", 0, 1)
         I("V", "zb", 0, 1)
         both_T(4, 0)
+        Z("zb", 0, 0)
         C("S", 4, 0)
         C("S", 4, 1)
-        Z("zb", 0, 0)
         bank_product(2, 2)
         I("V", "za", 0, 0)
         I("S", "za", 0, 0)
         Z("zb", 0, 1)
+        QM(4)
+        I("V", "zb", 1, 0)
+        I("S", "zb", 1, 0)
+        I("V", "zb", 1, 1)
+        I("S", "zb", 1, 1)
         Z("za", 0, 0)
         for i in range(3):
             L(i, 0, 0)
             L(i, 1, 0)
-        I("S", "zb", 1, 0)
-        I("V", "zb", 1, 0)
-        I("S", "zb", 1, 1)
-        I("V", "zb", 1, 1)
-        Z("zb", 1, 0)
-        bank_product(3, 0)
-        W("G", 0)
-        I("S", "za", 1, 0)
         I("V", "za", 1, 0)
+        I("S", "za", 1, 0)
+        bank_product(3, 0)
+        W(0)
+        W(1)
+        Z("zb", 1, 0)
         Z("zb", 1, 1)
         Z("za", 1, 0)
         L(3, 0, 0)
         L(3, 1, 0)
-        QM(4)
-        W("G", 1)
+        W(2)
         I("S", "za", 0, 1, 0)
         for i in range(4):
             L(i, 0, 1)
@@ -296,7 +295,6 @@ def tile_barlow_twins_bank_s1_kernel(tc, za, zb, ma, mb_words, mb_scales, ra, rb
         E(0, 0)
         E(0, 1)
         store(0)
-        W("G", 2)
         I("S", "za", 1, 1, 0)
         E(1, 0)
         E(1, 1)
@@ -304,46 +302,47 @@ def tile_barlow_twins_bank_s1_kernel(tc, za, zb, ma, mb_words, mb_scales, ra, rb
         both_T(5, 4)
         C("S", 5, 0)
         C("S", 5, 1)
-        Z("za", 0, 1)
-        bank_product(4, 6)
-        W("G", 3)
         E(2, 0)
         E(2, 1)
         store(2)
-        Z("za", 1, 1)
-        QM(5)
-        W("G", 4)
-        both_T(6, 2)
-        C("S", 6, 0)
-        C("S", 6, 1)
+        bank_product(4, 6)
+        W(3)
+        Z("za", 0, 1)
         E(3, 0)
         E(3, 1)
         store(3)
+        both_T(6, 2)
+        C("S", 6, 0)
+        C("S", 6, 1)
+        Z("za", 1, 1)
+        QM(5)
         for h in halves(4):
             L(4, h, 0)
             L(4, h, 1)
-        W("V", 6)
         QM(6)
-        W("G", 5)
         bank_product(5, 0)
+        W(4)
         for h in halves(4):
             E(4, h)
         store(4)
+        W(5)
         for h in halves(5):
             L(5, h, 0)
             L(5, h, 1)
-        W("V", 7)
         both_T(7, 4)
         C("S", 7, 0)
         C("S", 7, 1)
         for h in halves(5):
             E(5, h)
         store(5)
+        W(6)
         QM(7)
         bank_product(6, 6)
         for h in halves(6):
             L(6, h, 0)
             L(6, h, 1)
+        W(7)
+        for h in halves(6):
             E(6, h)
         store(6)
         bank_product(7, 2)

@@ -18,7 +18,7 @@ P = 128
 N = 512
 KP = 512
 FLOPS = 2 * D * D * (B + Q)
-V_COLS = 192
+V_COLS = 256
 
 
 def tile_barlow_twins_bank_s1_kernel(tc, za, zb, ma, mb_words, mb_scales, ra, rb, goal, pair, out):
@@ -69,47 +69,55 @@ def tile_barlow_twins_bank_s1_kernel(tc, za, zb, ma, mb_words, mb_scales, ra, rb
         def load_pair(a):
             nc.sync.dma_start(out=pair_sb[a][:], in_=pair_v[a])
 
-        nc.vector.memset(mbs[:].rearrange("p g n -> p (g n)").bitcast(I32), 0)
         nc.vector.memset(vec[:], 0.0)
-        for q in range(4):
-            nc.scalar.dma_start(
-                out=mbs[32 * q : 32 * q + 4, :, :].bitcast(I32),
-                in_=mb_scales[:, 4 * q : 4 * q + 4, :].bitcast(I32).rearrange("g r n -> r g n"),
-            )
+        for v, src in enumerate((ra, rb, goal)):
+            nc.scalar.dma_start(out=vec[8 * v : 8 * v + 8, :], in_=src.rearrange("(c p) -> c p", p=P))
+        nc.vector.memset(mbs[:].rearrange("p g n -> p (g n)").bitcast(I32), 0)
         make_identity(nc, ident[:])
         nc.vector.tensor_copy(out=ident_bf[:], in_=ident[:])
 
-        load_ma(0, 0, D)
-        load_ma(0, D, Q)
-        load_mb(0)
+        load_ma(0)
         load_ma(1)
-        for v, src in enumerate((ra, rb, goal)):
-            nc.scalar.dma_start(out=vec[8 * v : 8 * v + 8, :], in_=src.rearrange("(c p) -> c p", p=P))
-        load_mb(1)
         load_ma(2)
+        for q in range(4):
+            nc.sync.dma_start(
+                out=mbs[32 * q : 32 * q + 4, :, :].bitcast(I32),
+                in_=mb_scales[:, 4 * q : 4 * q + 4, :].bitcast(I32).rearrange("g r n -> r g n"),
+            )
         load_ma(3)
+        load_mb(0)
+        load_mb(1)
         load_zb(0)
-        load_ma(4)
         load_za(0, 0)
         load_zb(1)
         load_za(1, 0)
-        load_pair(0)
-        load_pair(1)
-        load_za(0, 1)
+        load_ma(4)
         load_ma(5)
+        load_pair(0)
+        load_za(0, 1)
         load_za(1, 1)
         load_ma(6)
-        load_pair(2)
+        load_pair(1)
         load_ma(7)
+        load_pair(2)
         load_pair(3)
 
         turned = {}
         grouped = {}
         zgrouped = {}
         acc = {}
-        weight = {}
         result = {}
-        diag = {}
+
+        sorted_words = {}
+
+        def X(eng, i):
+            w = stage.tile([P, 4, 2, P], F32, name="words%d" % i, tag="words", align_bytes=64)
+            sorted_words[i] = w
+            src = ma_raw[i][:].bitcast(F32).rearrange("p (g m u) -> p g u m", g=4, u=2)
+            if eng == "S":
+                nc.scalar.copy(out=w[:], in_=src)
+            else:
+                nc.vector.tensor_copy(out=w[:], in_=src)
 
         def T(i, b, bank):
             t = psum.tile([P, 2, 2, P], F32, name="turned%d_%d" % (i, b), tag="bank%d" % bank)
@@ -118,7 +126,11 @@ def tile_barlow_twins_bank_s1_kernel(tc, za, zb, ma, mb_words, mb_scales, ra, rb
             for gg in range(2):
                 g = 2 * b + gg
                 for u in range(2):
-                    nc.tensor.transpose(t[:, gg, u, :], words[:, 256 * g + u : 256 * (g + 1) : 2], ident[:])
+                    if i in sorted_words:
+                        src = sorted_words[i][:, g, u, :]
+                    else:
+                        src = words[:, 256 * g + u : 256 * (g + 1) : 2]
+                    nc.tensor.transpose(t[:, gg, u, :], src, ident[:])
 
         def C(eng, i, b):
             if i not in grouped:
@@ -181,47 +193,52 @@ def tile_barlow_twins_bank_s1_kernel(tc, za, zb, ma, mb_words, mb_scales, ra, rb
                 stop=(g == 1),
             )
 
-        def W(i):
-            w = stage.tile([P, D], F32, name="weight%d" % i, tag="weight", bufs=6, align_bytes=64)
-            weight[i] = w
-            src = pair_sb[i // 2][:, i % 2, :]
-            nc.vector.tensor_tensor(out=w[:], in0=src, in1=rb_all[:], op=MULT)
-            d = stage.tile([P, P], F32, name="diag%d" % i, tag="diag", align_bytes=64)
-            diag[i] = d
-            nc.gpsimd.tensor_tensor(out=d[:], in0=src[:, P * i : P * (i + 1)], in1=goal_diag[:, i, :], op=MULT)
-
         def E(i, h):
             if i not in result:
-                result[i] = stage.tile([P, D], F32, name="result%d" % i, tag="result", bufs=6, align_bytes=64)
+                result[i] = stage.tile([P, D], F32, name="result%d" % i, tag="result", bufs=5, align_bytes=64)
             c = slice(N * h, N * (h + 1))
             nc.vector.scalar_tensor_tensor(
-                out=result[i][:, c], in0=acc[i, h][:], scalar=cols[:, i : i + 1], in1=weight[i][:, c], op0=MULT, op1=MULT
+                out=result[i][:, c], in0=acc[i, h][:], scalar=cols[:, i : i + 1], in1=rb_all[:, c], op0=MULT, op1=MULT
             )
             if h == i // 4:
                 blk = result[i][:, P * i : P * (i + 1)]
-                nc.gpsimd.tensor_tensor(out=blk, in0=blk, in1=diag[i][:], op=SUB)
+                nc.gpsimd.tensor_tensor(out=blk, in0=blk, in1=goal_diag[:, i, :], op=SUB)
+
+        def M(eng, i, h):
+            c = slice(N * h, N * (h + 1))
+            e = nc.gpsimd if eng == "G" else nc.vector
+            e.tensor_tensor(out=result[i][:, c], in0=result[i][:, c], in1=pair_sb[i // 2][:, i % 2, c], op=MULT)
+
+        def finish(i):
+            for h in halves(i):
+                E(i, h)
+            for h in reversed(halves(i)) if i >= 5 else halves(i):
+                M("G" if i < 5 else "V", i, h)
+            store(i)
 
         def store(i, h=None):
             c = slice(0, D) if h is None else slice(N * h, N * (h + 1))
             nc.sync.dma_start(out=out[P * i : P * (i + 1), c], in_=result[i][:, c])
 
         def vectors():
-            t = psum.tile([P, P], BF16, name="vec_t", tag="bank6")
+            t = psum.tile([P, P], BF16, name="vec_t", tag="bank4")
             nc.tensor.transpose(t[:], vec[:], ident_bf[:])
             nc.vector.tensor_copy(out=rb_col[:], in_=t[:, 8:16])
             nc.vector.tensor_copy(out=cols[:], in_=t[:, 0:24])
-            nc.vector.tensor_tensor(
-                out=goal_diag[:],
-                in0=ident[:].unsqueeze(1).to_broadcast([P, 8, P]),
-                in1=cols[:, 16:24].unsqueeze(2).to_broadcast([P, 8, P]),
-                op=MULT,
-            )
 
         def spread_rb():
             t = psum.tile([P, D], BF16, name="rb_t", tag="bank7")
             for c in range(8):
                 nc.tensor.transpose(t[:, P * c : P * (c + 1)], rb_col[:, c : c + 1].to_broadcast([P, P]), ident_bf[:])
             nc.scalar.copy(out=rb_all[:], in_=t[:])
+
+        def make_goal_diag():
+            nc.vector.tensor_tensor(
+                out=goal_diag[:],
+                in0=ident[:].unsqueeze(1).to_broadcast([P, 8, P]),
+                in1=cols[:, 16:24].unsqueeze(2).to_broadcast([P, 8, P]),
+                op=MULT,
+            )
 
         def halves(i):
             return (1, 0) if i >= 4 else (0, 1)
@@ -236,118 +253,102 @@ def tile_barlow_twins_bank_s1_kernel(tc, za, zb, ma, mb_words, mb_scales, ra, rb
 
         both_T(0, 0)
         C("S", 0, 0)
-        C("V", 0, 1)
         QM(0, 0, 2)
+        X("V", 1)
+        C("V", 0, 1)
+        vectors()
         QM(0, 2, 4)
-        bank_product(0, 4, (0, 1))
         both_T(1, 2)
         C("S", 1, 0)
+        X("V", 2)
         C("V", 1, 1)
-        bank_product(0, 4, (2, 3))
-        QM(1)
-        vectors()
-        both_T(2, 0)
         spread_rb()
+        QM(1)
+        both_T(2, 4)
         C("S", 2, 0)
+        X("V", 3)
         C("V", 2, 1)
-        both_T(3, 2)
-        C("S", 3, 0)
         QM(2)
+        both_T(3, 6)
+        C("S", 3, 0)
         C("V", 3, 1)
-        bank_product(1, 6)
+        bank_product(0, 0)
+        make_goal_diag()
+        QM(3)
+        bank_product(1, 2)
+        bank_product(2, 4)
         I("S", "zb", 0, 0)
         I("V", "zb", 0, 0)
-        QM(3)
         I("S", "zb", 0, 1)
         I("V", "zb", 0, 1)
-        both_T(4, 0)
         Z("zb", 0, 0)
-        C("S", 4, 0)
-        C("S", 4, 1)
-        bank_product(2, 2)
-        I("V", "za", 0, 0)
         I("S", "za", 0, 0)
+        I("V", "za", 0, 0)
         Z("zb", 0, 1)
-        QM(4)
-        I("V", "zb", 1, 0)
-        I("S", "zb", 1, 0)
-        I("V", "zb", 1, 1)
-        I("S", "zb", 1, 1)
+        bank_product(3, 6)
         Z("za", 0, 0)
-        for i in range(3):
-            L(i, 0, 0)
-            L(i, 1, 0)
-        I("V", "za", 1, 0)
-        I("S", "za", 1, 0)
-        bank_product(3, 0)
-        W(0)
-        W(1)
+        I("S", "zb", 1, 0)
+        I("V", "zb", 1, 0)
+        I("S", "zb", 1, 1)
+        I("V", "zb", 1, 1)
         Z("zb", 1, 0)
+        I("S", "za", 1, 0)
+        I("V", "za", 1, 0)
         Z("zb", 1, 1)
         Z("za", 1, 0)
-        L(3, 0, 0)
-        L(3, 1, 0)
-        W(2)
-        I("S", "za", 0, 1, 0)
+        for i in range(4):
+            L(i, 0, 0)
+            L(i, 1, 0)
+        X("S", 4)
+        X("S", 5)
         for i in range(4):
             L(i, 0, 1)
             L(i, 1, 1)
-        E(0, 0)
-        E(0, 1)
-        store(0)
-        I("S", "za", 1, 1, 0)
-        E(1, 0)
-        E(1, 1)
-        store(1)
-        both_T(5, 4)
+        finish(0)
+        finish(1)
+        both_T(4, 0)
+        C("S", 4, 0)
+        C("V", 4, 1)
+        both_T(5, 2)
         C("S", 5, 0)
+        QM(4)
+        finish(2)
         C("S", 5, 1)
-        E(2, 0)
-        E(2, 1)
-        store(2)
-        bank_product(4, 6)
-        W(3)
-        Z("za", 0, 1)
-        E(3, 0)
-        E(3, 1)
-        store(3)
-        both_T(6, 2)
-        C("S", 6, 0)
-        C("S", 6, 1)
-        Z("za", 1, 1)
+        finish(3)
         QM(5)
+        bank_product(4, 4)
+        I("S", "za", 0, 1, 0)
+        X("S", 6)
+        Z("za", 0, 1)
+        I("S", "za", 1, 1, 0)
+        X("S", 7)
+        both_T(6, 0)
+        both_T(7, 2)
+        Z("za", 1, 1)
+        bank_product(5, 6)
+        for b in range(2):
+            C("S", 6, b)
+        QM(6)
+        for b in range(2):
+            C("S", 7, b)
         for h in halves(4):
             L(4, h, 0)
             L(4, h, 1)
-        QM(6)
-        bank_product(5, 0)
-        W(4)
-        for h in halves(4):
-            E(4, h)
-        store(4)
-        W(5)
+        finish(4)
+        QM(7)
         for h in halves(5):
             L(5, h, 0)
             L(5, h, 1)
-        both_T(7, 4)
-        C("S", 7, 0)
-        C("S", 7, 1)
-        for h in halves(5):
-            E(5, h)
-        store(5)
-        W(6)
-        QM(7)
-        bank_product(6, 6)
+        finish(5)
+        bank_product(6, 0)
         for h in halves(6):
             L(6, h, 0)
             L(6, h, 1)
-        W(7)
-        for h in halves(6):
-            E(6, h)
-        store(6)
+        finish(6)
         bank_product(7, 2)
         for h in halves(7):
             L(7, h, 0)
             L(7, h, 1)
             E(7, h)
+            M("V", 7, h)
             store(7, h)

@@ -69,40 +69,24 @@ def tile_barlow_twins_bank_s1_kernel(tc, za, zb, ma, mb_words, mb_scales, ra, rb
         def load_pair(a):
             nc.sync.dma_start(out=pair_sb[a][:], in_=pair_v[a])
 
-        nc.vector.memset(vec[:], 0.0)
-        for v, src in enumerate((ra, rb, goal)):
-            nc.scalar.dma_start(out=vec[8 * v : 8 * v + 8, :], in_=src.rearrange("(c p) -> c p", p=P))
+        nc.gpsimd.memset(vec[:], 0.0)
         nc.vector.memset(mbs[:].rearrange("p g n -> p (g n)").bitcast(I32), 0)
         make_identity(nc, ident[:])
         nc.vector.tensor_copy(out=ident_bf[:], in_=ident[:])
 
-        load_ma(0)
-        load_ma(1)
-        load_ma(2)
-        for q in range(4):
-            nc.sync.dma_start(
-                out=mbs[32 * q : 32 * q + 4, :, :].bitcast(I32),
-                in_=mb_scales[:, 4 * q : 4 * q + 4, :].bitcast(I32).rearrange("g r n -> r g n"),
-            )
-        load_ma(3)
-        load_mb(0)
-        load_mb(1)
-        load_zb(0)
-        load_za(0, 0)
-        load_zb(1)
-        load_za(1, 0)
-        load_ma(4)
-        load_ma(5)
-        load_pair(0)
-        load_za(0, 1)
-        load_za(1, 1)
-        load_ma(6)
-        load_pair(1)
-        load_ma(7)
-        load_pair(2)
-        load_pair(3)
+        def load_vectors():
+            for v, src in enumerate((ra, rb, goal)):
+                nc.sync.dma_start(out=vec[8 * v : 8 * v + 8, :], in_=src.rearrange("(c p) -> c p", p=P))
+
+        def load_scales():
+            for q in range(4):
+                nc.sync.dma_start(
+                    out=mbs[32 * q : 32 * q + 4, :, :].bitcast(I32),
+                    in_=mb_scales[:, 4 * q : 4 * q + 4, :].bitcast(I32).rearrange("g r n -> r g n"),
+                )
 
         turned = {}
+        small = {}
         grouped = {}
         zgrouped = {}
         acc = {}
@@ -182,6 +166,13 @@ def tile_barlow_twins_bank_s1_kernel(tc, za, zb, ma, mb_words, mb_scales, ra, rb
                     stop=False,
                 )
 
+        def TT(i, bank):
+            T(i, 0, bank)
+            T(i, 1, bank + 1)
+
+        def B(i, h, bank):
+            bank_pass(i, h, (0, 1, 2, 3), bank)
+
         def L(i, h, g):
             nc.tensor.matmul_mx(
                 out=acc[i, h][:],
@@ -198,39 +189,49 @@ def tile_barlow_twins_bank_s1_kernel(tc, za, zb, ma, mb_words, mb_scales, ra, rb
                 result[i] = stage.tile([P, D], F32, name="result%d" % i, tag="result", bufs=5, align_bytes=64)
             c = slice(N * h, N * (h + 1))
             nc.vector.scalar_tensor_tensor(
-                out=result[i][:, c], in0=acc[i, h][:], scalar=cols[:, i : i + 1], in1=rb_all[:, c], op0=MULT, op1=MULT
+                out=result[i][:, c], in0=acc[i, h][:], scalar=cols[:, i : i + 1], in1=weight[i][:, c] if i in weight else rb_all[:, c], op0=MULT, op1=MULT
             )
+
+        def G(i, h):
             if h == i // 4:
                 blk = result[i][:, P * i : P * (i + 1)]
-                nc.gpsimd.tensor_tensor(out=blk, in0=blk, in1=goal_diag[:, i, :], op=SUB)
+                nc.gpsimd.tensor_tensor(out=blk, in0=blk, in1=diag[i][:] if i in diag else goal_diag[:, i, :], op=SUB)
+            if i not in weight:
+                M(i, h)
 
-        def M(eng, i, h):
+        weight = {}
+        diag = {}
+
+        def W(i):
+            weight[i] = stage.tile([P, D], F32, name="weight%d" % i, tag="weight", bufs=4, align_bytes=64)
+            src = pair_sb[i // 2][:, i % 2, :]
+            nc.vector.tensor_tensor(out=weight[i][:], in0=src, in1=rb_all[:], op=MULT)
+            diag[i] = stage.tile([P, P], F32, name="diag%d" % i, tag="diag", bufs=4, align_bytes=64)
+            nc.gpsimd.tensor_tensor(out=diag[i][:], in0=src[:, P * i : P * (i + 1)], in1=goal_diag[:, i, :], op=MULT)
+
+        def M(i, h):
             c = slice(N * h, N * (h + 1))
-            e = nc.gpsimd if eng == "G" else nc.vector
-            e.tensor_tensor(out=result[i][:, c], in0=result[i][:, c], in1=pair_sb[i // 2][:, i % 2, c], op=MULT)
-
-        def finish(i):
-            for h in halves(i):
-                E(i, h)
-            for h in reversed(halves(i)) if i >= 5 else halves(i):
-                M("G" if i < 5 else "V", i, h)
-            store(i)
+            nc.gpsimd.tensor_tensor(out=result[i][:, c], in0=result[i][:, c], in1=pair_sb[i // 2][:, i % 2, c], op=MULT)
 
         def store(i, h=None):
             c = slice(0, D) if h is None else slice(N * h, N * (h + 1))
             nc.sync.dma_start(out=out[P * i : P * (i + 1), c], in_=result[i][:, c])
 
-        def vectors():
-            t = psum.tile([P, P], BF16, name="vec_t", tag="bank4")
-            nc.tensor.transpose(t[:], vec[:], ident_bf[:])
-            nc.vector.tensor_copy(out=rb_col[:], in_=t[:, 8:16])
-            nc.vector.tensor_copy(out=cols[:], in_=t[:, 0:24])
+        def vec_turn():
+            small["vec"] = psum.tile([P, P], BF16, name="vec_t", tag="bank4")
+            nc.tensor.transpose(small["vec"][:], vec[:], ident_bf[:])
 
-        def spread_rb():
-            t = psum.tile([P, D], BF16, name="rb_t", tag="bank7")
+        def vec_take():
+            nc.vector.tensor_copy(out=rb_col[:], in_=small["vec"][:, 8:16])
+            nc.vector.tensor_copy(out=cols[:], in_=small["vec"][:, 0:24])
+
+        def rb_turn():
+            small["rb"] = psum.tile([P, D], BF16, name="rb_t", tag="bank7")
             for c in range(8):
-                nc.tensor.transpose(t[:, P * c : P * (c + 1)], rb_col[:, c : c + 1].to_broadcast([P, P]), ident_bf[:])
-            nc.scalar.copy(out=rb_all[:], in_=t[:])
+                nc.tensor.transpose(small["rb"][:, P * c : P * (c + 1)], rb_col[:, c : c + 1].to_broadcast([P, P]), ident_bf[:])
+
+        def rb_take():
+            nc.scalar.copy(out=rb_all[:], in_=small["rb"][:])
 
         def make_goal_diag():
             nc.vector.tensor_tensor(
@@ -240,115 +241,209 @@ def tile_barlow_twins_bank_s1_kernel(tc, za, zb, ma, mb_words, mb_scales, ra, rb
                 op=MULT,
             )
 
-        def halves(i):
-            return (1, 0) if i >= 4 else (0, 1)
-
-        def both_T(i, bank):
-            T(i, 0, bank)
-            T(i, 1, bank + 1)
-
-        def bank_product(i, bank, gs=(0, 1, 2, 3)):
-            for h in halves(i):
-                bank_pass(i, h, gs, bank + h)
-
-        both_T(0, 0)
-        C("S", 0, 0)
-        QM(0, 0, 2)
-        X("V", 1)
-        C("V", 0, 1)
-        vectors()
-        QM(0, 2, 4)
-        both_T(1, 2)
-        C("S", 1, 0)
-        X("V", 2)
-        C("V", 1, 1)
-        spread_rb()
-        QM(1)
-        both_T(2, 4)
-        C("S", 2, 0)
-        X("V", 3)
-        C("V", 2, 1)
-        QM(2)
-        both_T(3, 6)
-        C("S", 3, 0)
-        C("V", 3, 1)
-        bank_product(0, 0)
+        load_ma(0)
+        T(0, 1, 1)
+        load_vectors()
+        C("S", 0, 1)
+        load_ma(2)
+        vec_turn()
+        load_zb(0)
+        vec_take()
+        load_ma(1)
+        T(0, 0, 0)
         make_goal_diag()
-        QM(3)
-        bank_product(1, 2)
-        bank_product(2, 4)
-        I("S", "zb", 0, 0)
-        I("V", "zb", 0, 0)
-        I("S", "zb", 0, 1)
-        I("V", "zb", 0, 1)
-        Z("zb", 0, 0)
-        I("S", "za", 0, 0)
-        I("V", "za", 0, 0)
+        T(2, 0, 4)
+        load_scales()
+        C("S", 0, 0)
+        QM(0)
+        T(2, 1, 5)
+        C("S", 2, 1)
+        load_mb(0)
+        load_ma(3)
+        rb_turn()
+        I("S", "zb", 0, 1, 384)
+        T(1, 0, 2)
+        I("S", "zb", 0, 0, 448)
+        T(1, 1, 3)
+        I("V", "zb", 0, 1, 384)
+        I("V", "zb", 0, 0, 448)
+        load_za(0, 0)
+        load_zb(1)
+        C("S", 2, 0)
+        rb_take()
         Z("zb", 0, 1)
-        bank_product(3, 6)
+        QM(2)
+        bank_pass(0, 1, (0, 1), 1)
+        C("S", 1, 1)
+        T(3, 0, 6)
+        load_mb(1)
+        load_za(1, 0)
+        Z("zb", 0, 0)
+        C("S", 1, 0)
+        C("S", 3, 0)
+        T(3, 1, 7)
+        I("S", "za", 0, 0, 384)
+        QM(1)
+        I("V", "za", 0, 0, 384)
+        bank_pass(2, 0, (0, 1), 4)
+        C("S", 3, 1)
         Z("za", 0, 0)
-        I("S", "zb", 1, 0)
-        I("V", "zb", 1, 0)
-        I("S", "zb", 1, 1)
-        I("V", "zb", 1, 1)
+        load_pair(0)
+        bank_pass(0, 0, (0, 1), 0)
+        bank_pass(1, 1, (0, 1), 3)
+        load_ma(4)
+        load_ma(5)
+        bank_pass(2, 1, (0, 1), 5)
+        bank_pass(1, 0, (0, 1), 2)
+        QM(3)
+        I("S", "zb", 1, 1, 256)
+        bank_pass(3, 0, (0, 1), 6)
+        bank_pass(3, 1, (0, 1), 7)
+        I("V", "zb", 1, 1, 256)
+        bank_pass(0, 1, (2, 3), 1)
+        I("V", "zb", 1, 0, 320)
+        I("S", "zb", 1, 0, 320)
+        I("S", "za", 1, 0, 64)
+        I("V", "za", 1, 0, 64)
+        bank_pass(1, 0, (2, 3), 2)
+        bank_pass(0, 0, (2, 3), 0)
+        L(1, 0, 0)
         Z("zb", 1, 0)
-        I("S", "za", 1, 0)
-        I("V", "za", 1, 0)
+        bank_pass(2, 0, (2, 3), 4)
+        bank_pass(1, 1, (2, 3), 3)
+        L(0, 1, 0)
         Z("zb", 1, 1)
-        Z("za", 1, 0)
-        for i in range(4):
-            L(i, 0, 0)
-            L(i, 1, 0)
         X("S", 4)
+        load_za(0, 1)
+        L(2, 0, 0)
         X("S", 5)
-        for i in range(4):
-            L(i, 0, 1)
-            L(i, 1, 1)
-        finish(0)
-        finish(1)
-        both_T(4, 0)
-        C("S", 4, 0)
-        C("V", 4, 1)
-        both_T(5, 2)
-        C("S", 5, 0)
-        QM(4)
-        finish(2)
-        C("S", 5, 1)
-        finish(3)
-        QM(5)
-        bank_product(4, 4)
+        L(1, 1, 0)
+        W(1)
+        load_pair(1)
+        Z("za", 1, 0)
+        W(0)
+        L(1, 0, 1)
+        E(1, 0)
+        L(2, 0, 1)
+        load_ma(6)
+        G(1, 0)
+        L(0, 0, 0)
+        load_ma(7)
         I("S", "za", 0, 1, 0)
-        X("S", 6)
-        Z("za", 0, 1)
-        I("S", "za", 1, 1, 0)
+        L(1, 1, 1)
+        L(0, 0, 1)
+        E(0, 0)
+        L(0, 1, 1)
+        bank_pass(3, 0, (2, 3), 6)
+        bank_pass(2, 1, (2, 3), 5)
+        E(1, 1)
+        L(2, 1, 0)
+        T(4, 0, 0)
+        T(5, 0, 2)
+        E(0, 1)
+        T(4, 1, 1)
+        W(2)
+        C("S", 4, 0)
+        X("V", 6)
+        T(5, 1, 3)
+        bank_pass(3, 1, (2, 3), 7)
+        C("S", 4, 1)
+        load_za(1, 1)
+        E(2, 0)
+        C("S", 5, 0)
+        W(3)
+        L(3, 0, 0)
+        QM(4)
+        L(3, 1, 0)
+        L(2, 1, 1)
         X("S", 7)
-        both_T(6, 0)
-        both_T(7, 2)
+        C("S", 5, 1)
+        load_pair(3)
+        L(3, 0, 1)
+        I("S", "za", 1, 1, 0)
+        G(2, 0)
+        E(3, 0)
+        L(3, 1, 1)
+        T(6, 1, 1)
+        T(6, 0, 0)
+        QM(5)
+        T(7, 0, 2)
+        G(3, 0)
+        T(7, 1, 3)
+        C("S", 7, 1)
+        bank_pass(4, 1, (0, 1), 4)
+        Z("za", 0, 1)
+        load_pair(2)
+        store(1)
+        E(3, 1)
+        bank_pass(4, 1, (2, 3), 4)
+        E(2, 1)
+        G(2, 1)
+        bank_pass(5, 1, (0, 1), 6)
         Z("za", 1, 1)
-        bank_product(5, 6)
-        for b in range(2):
-            C("S", 6, b)
+        bank_pass(5, 1, (2, 3), 6)
+        C("S", 6, 1)
+        C("S", 6, 0)
+        L(4, 1, 0)
+        L(5, 1, 0)
+        G(0, 0)
+        W(6)
+        bank_pass(4, 0, (0, 1), 5)
+        L(4, 1, 1)
+        store(3)
         QM(6)
-        for b in range(2):
-            C("S", 7, b)
-        for h in halves(4):
-            L(4, h, 0)
-            L(4, h, 1)
-        finish(4)
+        C("S", 7, 0)
+        W(5)
+        bank_pass(5, 0, (0, 1), 7)
+        bank_pass(4, 0, (2, 3), 5)
+        G(5, 0)
+        W(4)
+        bank_pass(5, 0, (2, 3), 7)
+        L(5, 1, 1)
+        G(0, 1)
+        E(5, 1)
+        bank_pass(6, 0, (0, 1), 1)
+        L(5, 0, 0)
+        bank_pass(6, 1, (0, 1), 0)
+        L(5, 0, 1)
+        G(5, 1)
+        E(4, 1)
+        G(1, 1)
         QM(7)
-        for h in halves(5):
-            L(5, h, 0)
-            L(5, h, 1)
-        finish(5)
-        bank_product(6, 0)
-        for h in halves(6):
-            L(6, h, 0)
-            L(6, h, 1)
-        finish(6)
-        bank_product(7, 2)
-        for h in halves(7):
-            L(7, h, 0)
-            L(7, h, 1)
-            E(7, h)
-            M("V", 7, h)
-            store(7, h)
+        bank_pass(6, 0, (2, 3), 1)
+        bank_pass(6, 1, (2, 3), 0)
+        store(2)
+        L(6, 1, 0)
+        L(6, 1, 1)
+        L(4, 0, 0)
+        L(4, 0, 1)
+        G(3, 1)
+        L(6, 0, 0)
+        bank_pass(7, 1, (0, 1), 2)
+        E(5, 0)
+        bank_pass(7, 1, (2, 3), 2)
+        G(6, 0)
+        G(4, 0)
+        store(0)
+        E(6, 1)
+        L(6, 0, 1)
+        G(4, 1)
+        L(7, 1, 0)
+        L(7, 1, 1)
+        bank_pass(7, 0, (0, 1), 3)
+        G(6, 1)
+        E(4, 0)
+        bank_pass(7, 0, (2, 3), 3)
+        store(5)
+        W(7)
+        E(6, 0)
+        E(7, 1)
+        L(7, 0, 0)
+        store(4)
+        G(7, 1)
+        L(7, 0, 1)
+        store(6)
+        store(7, 1)
+        E(7, 0)
+        store(7, 0)
+        G(7, 0)

@@ -35,15 +35,14 @@ def tile_barlow_twins_bank_s1_kernel(tc, za, zb, ma, mb_words, mb_scales, ra, rb
         cols = keep.tile([P, 24], F32, name="cols", align_bytes=64)
         rb_col = keep.tile([P, 8], BF16, name="rb_col", align_bytes=64)
         rb_all = keep.tile([P, D], BF16, name="rb_all", align_bytes=64)
-        goal_diag = keep.tile([P, 8, P], F32, name="goal_diag", align_bytes=64)
-        mbw = keep.tile([P, 4, 2 * D], U8, name="mbw", align_bytes=64)
-        mbs = keep.tile([P, 4, D], U8, name="mbs", align_bytes=64)
-        za_codes = keep.tile([P, 2, D], U32, name="za_codes", align_bytes=64)
-        za_scales = keep.tile([P, 2, D], U8, name="za_scales", align_bytes=64)
-        zb_codes = keep.tile([P, 2, D], U32, name="zb_codes", align_bytes=64)
-        zb_scales = keep.tile([P, 2, D], U8, name="zb_scales", align_bytes=64)
-        ma_codes = [keep.tile([P, 4, P], U32, name="ma_codes%d" % i, align_bytes=64) for i in range(8)]
-        ma_scales = [keep.tile([P, 4, P], U8, name="ma_scales%d" % i, align_bytes=64) for i in range(8)]
+        mbw = keep.tile([P, 4, 2 * D], U8, name="mbw", align_bytes=256)
+        mbs = keep.tile([P, 4, D], U8, name="mbs", align_bytes=256)
+        za_codes = keep.tile([P, 2, D], U32, name="za_codes", align_bytes=256)
+        za_scales = keep.tile([P, 2, D], U8, name="za_scales", align_bytes=256)
+        zb_codes = keep.tile([P, 2, D], U32, name="zb_codes", align_bytes=256)
+        zb_scales = keep.tile([P, 2, D], U8, name="zb_scales", align_bytes=256)
+        ma_codes = [keep.tile([P, 4, P], U32, name="ma_codes%d" % i, align_bytes=256) for i in range(8)]
+        ma_scales = [keep.tile([P, 4, P], U8, name="ma_scales%d" % i, align_bytes=256) for i in range(8)]
         ma_raw = [keep.tile([P, Q], BF16, name="ma_raw%d" % i, align_bytes=64) for i in range(8)]
         zb_raw = [keep.tile([P, 4, D], BF16, name="zb_raw%d" % g, align_bytes=64) for g in range(2)]
         za_raw = [[keep.tile([P, 4, N], BF16, name="za_raw%d%d" % (g, h), align_bytes=64) for h in range(2)] for g in range(2)]
@@ -140,9 +139,15 @@ def tile_barlow_twins_bank_s1_kernel(tc, za, zb, ma, mb_words, mb_scales, ra, rb
             dst = zgrouped[z, g, h]
             src = zb_raw[g][:, :, N * h : N * (h + 1)] if z == "zb" else za_raw[g][h][:]
             if eng == "V":
-                nc.vector.tensor_copy(out=dst[:, 0:v_cols, :], in_=src[:, :, 0:v_cols].rearrange("p j w -> p w j"))
+                nc.vector.tensor_copy(
+                    out=dst[:, 0:v_cols, :].rearrange("p (c i) j -> p c j i", i=4),
+                    in_=src[:, :, 0:v_cols].rearrange("p j (c i) -> p c j i", i=4),
+                )
             else:
-                nc.scalar.copy(out=dst[:, v_cols:N, :], in_=src[:, :, v_cols:N].rearrange("p j w -> p w j"))
+                nc.scalar.copy(
+                    out=dst[:, v_cols:N, :].rearrange("p (c i) j -> p c j i", i=4),
+                    in_=src[:, :, v_cols:N].rearrange("p j (c i) -> p c j i", i=4),
+                )
 
         def Z(z, g, h):
             codes, scales = (zb_codes, zb_scales) if z == "zb" else (za_codes, za_scales)
@@ -189,15 +194,13 @@ def tile_barlow_twins_bank_s1_kernel(tc, za, zb, ma, mb_words, mb_scales, ra, rb
                 result[i] = stage.tile([P, D], F32, name="result%d" % i, tag="result", bufs=5, align_bytes=64)
             c = slice(N * h, N * (h + 1))
             nc.vector.scalar_tensor_tensor(
-                out=result[i][:, c], in0=acc[i, h][:], scalar=cols[:, i : i + 1], in1=weight[i][:, c] if i in weight else rb_all[:, c], op0=MULT, op1=MULT
+                out=result[i][:, c], in0=acc[i, h][:], scalar=cols[:, i : i + 1], in1=weight[i][:, c], op0=MULT, op1=MULT
             )
 
         def G(i, h):
             if h == i // 4:
                 blk = result[i][:, P * i : P * (i + 1)]
-                nc.gpsimd.tensor_tensor(out=blk, in0=blk, in1=diag[i][:] if i in diag else goal_diag[:, i, :], op=SUB)
-            if i not in weight:
-                M(i, h)
+                nc.gpsimd.tensor_tensor(out=blk, in0=blk, in1=diag[i][:], op=SUB)
 
         weight = {}
         diag = {}
@@ -206,12 +209,12 @@ def tile_barlow_twins_bank_s1_kernel(tc, za, zb, ma, mb_words, mb_scales, ra, rb
             weight[i] = stage.tile([P, D], F32, name="weight%d" % i, tag="weight", bufs=4, align_bytes=64)
             src = pair_sb[i // 2][:, i % 2, :]
             nc.vector.tensor_tensor(out=weight[i][:], in0=src, in1=rb_all[:], op=MULT)
-            diag[i] = stage.tile([P, P], F32, name="diag%d" % i, tag="diag", bufs=4, align_bytes=64)
-            nc.gpsimd.tensor_tensor(out=diag[i][:], in0=src[:, P * i : P * (i + 1)], in1=goal_diag[:, i, :], op=MULT)
 
-        def M(i, h):
-            c = slice(N * h, N * (h + 1))
-            nc.gpsimd.tensor_tensor(out=result[i][:, c], in0=result[i][:, c], in1=pair_sb[i // 2][:, i % 2, c], op=MULT)
+        def goal_term(i):
+            diag[i] = stage.tile([P, P], F32, name="diag%d" % i, tag="diag", bufs=4, align_bytes=64)
+            src = pair_sb[i // 2][:, i % 2, P * i : P * (i + 1)]
+            nc.scalar.activation(out=diag[i][:], in_=src, func=mybir.ActivationFunctionType.Copy, scale=cols[:, 16 + i : 17 + i])
+            nc.gpsimd.tensor_tensor(out=diag[i][:], in0=diag[i][:], in1=ident[:], op=MULT)
 
         def store(i, h=None):
             c = slice(0, D) if h is None else slice(N * h, N * (h + 1))
@@ -233,217 +236,209 @@ def tile_barlow_twins_bank_s1_kernel(tc, za, zb, ma, mb_words, mb_scales, ra, rb
         def rb_take():
             nc.scalar.copy(out=rb_all[:], in_=small["rb"][:])
 
-        def make_goal_diag():
-            nc.vector.tensor_tensor(
-                out=goal_diag[:],
-                in0=ident[:].unsqueeze(1).to_broadcast([P, 8, P]),
-                in1=cols[:, 16:24].unsqueeze(2).to_broadcast([P, 8, P]),
-                op=MULT,
-            )
-
-        load_ma(0)
-        T(0, 1, 1)
+        load_ma(0, 0, D)
         load_vectors()
-        C("S", 0, 1)
-        load_ma(2)
         vec_turn()
-        load_zb(0)
-        vec_take()
-        load_ma(1)
+        load_ma(0, D, Q)
         T(0, 0, 0)
-        make_goal_diag()
-        T(2, 0, 4)
-        load_scales()
-        C("S", 0, 0)
-        QM(0)
+        vec_take()
+        T(0, 1, 1)
+        C("V", 0, 0)
+        load_ma(2)
         T(2, 1, 5)
-        C("S", 2, 1)
-        load_mb(0)
-        load_ma(3)
+        C("S", 0, 1)
+        load_zb(0)
+        load_ma(1)
+        T(2, 0, 4)
         rb_turn()
-        I("S", "zb", 0, 1, 384)
-        T(1, 0, 2)
-        I("S", "zb", 0, 0, 448)
-        T(1, 1, 3)
-        I("V", "zb", 0, 1, 384)
-        I("V", "zb", 0, 0, 448)
-        load_za(0, 0)
-        load_zb(1)
+        load_mb(0)
+        C("V", 2, 1)
         C("S", 2, 0)
-        rb_take()
-        Z("zb", 0, 1)
+        I("S", "zb", 0, 0, 256)
+        QM(0)
         QM(2)
+        load_scales()
+        rb_take()
+        T(1, 0, 2)
+        I("V", "zb", 0, 0, 256)
+        I("V", "zb", 0, 1, 384)
+        load_ma(3)
+        load_za(0, 0)
+        Z("zb", 0, 0)
+        T(1, 1, 3)
         bank_pass(0, 1, (0, 1), 1)
         C("S", 1, 1)
+        I("S", "zb", 0, 1, 384)
         T(3, 0, 6)
-        load_mb(1)
-        load_za(1, 0)
-        Z("zb", 0, 0)
-        C("S", 1, 0)
-        C("S", 3, 0)
         T(3, 1, 7)
-        I("S", "za", 0, 0, 384)
-        QM(1)
-        I("V", "za", 0, 0, 384)
-        bank_pass(2, 0, (0, 1), 4)
-        C("S", 3, 1)
-        Z("za", 0, 0)
+        load_zb(1)
+        load_mb(1)
+        C("V", 1, 0)
+        load_za(1, 0)
+        C("S", 3, 0)
         load_pair(0)
+        QM(1)
+        Z("zb", 0, 1)
         bank_pass(0, 0, (0, 1), 0)
-        bank_pass(1, 1, (0, 1), 3)
-        load_ma(4)
-        load_ma(5)
-        bank_pass(2, 1, (0, 1), 5)
+        bank_pass(2, 0, (0, 1), 4)
         bank_pass(1, 0, (0, 1), 2)
+        I("V", "za", 0, 0, 384)
+        C("S", 3, 1)
+        load_ma(4)
+        I("S", "za", 0, 0, 384)
+        bank_pass(2, 1, (0, 1), 5)
         QM(3)
-        I("S", "zb", 1, 1, 256)
-        bank_pass(3, 0, (0, 1), 6)
-        bank_pass(3, 1, (0, 1), 7)
+        Z("za", 0, 0)
         I("V", "zb", 1, 1, 256)
-        bank_pass(0, 1, (2, 3), 1)
-        I("V", "zb", 1, 0, 320)
         I("S", "zb", 1, 0, 320)
-        I("S", "za", 1, 0, 64)
-        I("V", "za", 1, 0, 64)
-        bank_pass(1, 0, (2, 3), 2)
-        bank_pass(0, 0, (2, 3), 0)
-        L(1, 0, 0)
-        Z("zb", 1, 0)
-        bank_pass(2, 0, (2, 3), 4)
-        bank_pass(1, 1, (2, 3), 3)
-        L(0, 1, 0)
-        Z("zb", 1, 1)
-        X("S", 4)
+        bank_pass(3, 1, (0, 1), 7)
+        I("V", "zb", 1, 0, 320)
+        load_ma(5)
+        bank_pass(3, 0, (0, 1), 6)
         load_za(0, 1)
-        L(2, 0, 0)
-        X("S", 5)
-        L(1, 1, 0)
-        W(1)
+        bank_pass(1, 1, (0, 1), 3)
         load_pair(1)
-        Z("za", 1, 0)
-        W(0)
-        L(1, 0, 1)
-        E(1, 0)
-        L(2, 0, 1)
-        load_ma(6)
-        G(1, 0)
-        L(0, 0, 0)
-        load_ma(7)
-        I("S", "za", 0, 1, 0)
-        L(1, 1, 1)
-        L(0, 0, 1)
-        E(0, 0)
-        L(0, 1, 1)
-        bank_pass(3, 0, (2, 3), 6)
+        Z("zb", 1, 0)
+        bank_pass(1, 1, (2, 3), 3)
+        L(1, 1, 0)
+        bank_pass(0, 0, (2, 3), 0)
+        I("S", "zb", 1, 1, 256)
+        I("V", "za", 1, 0, 128)
         bank_pass(2, 1, (2, 3), 5)
-        E(1, 1)
-        L(2, 1, 0)
-        T(4, 0, 0)
-        T(5, 0, 2)
-        E(0, 1)
-        T(4, 1, 1)
-        W(2)
-        C("S", 4, 0)
-        X("V", 6)
-        T(5, 1, 3)
+        bank_pass(0, 1, (2, 3), 1)
+        bank_pass(1, 0, (2, 3), 2)
+        L(1, 0, 0)
+        Z("zb", 1, 1)
+        W(1)
+        bank_pass(2, 0, (2, 3), 4)
+        I("S", "za", 1, 0, 128)
+        L(0, 1, 0)
+        Z("za", 1, 0)
+        L(0, 0, 0)
+        L(1, 0, 1)
+        L(0, 0, 1)
+        W(0)
+        load_ma(6)
+        E(1, 0)
+        L(1, 1, 1)
         bank_pass(3, 1, (2, 3), 7)
-        C("S", 4, 1)
+        L(0, 1, 1)
+        E(0, 0)
+        goal_term(1)
+        E(0, 1)
+        bank_pass(3, 0, (2, 3), 6)
+        E(1, 1)
+        W(2)
+        X("S", 4)
+        load_ma(7)
+        L(2, 0, 0)
+        goal_term(0)
+        X("V", 6)
+        X("S", 5)
+        I("S", "za", 0, 1, 0)
+        L(2, 0, 1)
+        G(0, 0)
+        T(4, 1, 1)
         load_za(1, 1)
-        E(2, 0)
-        C("S", 5, 0)
-        W(3)
-        L(3, 0, 0)
-        QM(4)
-        L(3, 1, 0)
-        L(2, 1, 1)
-        X("S", 7)
-        C("S", 5, 1)
-        load_pair(3)
-        L(3, 0, 1)
-        I("S", "za", 1, 1, 0)
-        G(2, 0)
-        E(3, 0)
-        L(3, 1, 1)
-        T(6, 1, 1)
-        T(6, 0, 0)
-        QM(5)
-        T(7, 0, 2)
-        G(3, 0)
-        T(7, 1, 3)
-        C("S", 7, 1)
-        bank_pass(4, 1, (0, 1), 4)
-        Z("za", 0, 1)
+        T(4, 0, 0)
+        T(5, 1, 3)
+        C("S", 4, 0)
+        C("S", 4, 1)
         load_pair(2)
-        store(1)
-        E(3, 1)
+        E(2, 0)
+        T(5, 0, 2)
+        L(2, 1, 0)
+        L(3, 1, 0)
+        load_pair(3)
+        L(3, 1, 1)
+        QM(4)
+        L(3, 0, 0)
+        C("S", 5, 1)
+        W(3)
+        L(3, 0, 1)
+        G(1, 0)
+        T(6, 0, 0)
+        L(2, 1, 1)
+        bank_pass(4, 1, (0, 1), 4)
+        C("S", 5, 0)
+        QM(5)
         bank_pass(4, 1, (2, 3), 4)
+        X("S", 7)
+        store(1)
+        goal_term(2)
+        T(6, 1, 1)
+        store(0)
+        T(7, 1, 3)
+        T(7, 0, 2)
+        E(3, 0)
         E(2, 1)
-        G(2, 1)
-        bank_pass(5, 1, (0, 1), 6)
-        Z("za", 1, 1)
-        bank_pass(5, 1, (2, 3), 6)
+        E(3, 1)
+        G(2, 0)
+        goal_term(3)
         C("S", 6, 1)
+        bank_pass(5, 1, (0, 1), 6)
+        bank_pass(5, 1, (2, 3), 6)
+        bank_pass(5, 0, (0, 1), 7)
+        bank_pass(5, 0, (2, 3), 7)
+        Z("za", 0, 1)
         C("S", 6, 0)
+        QM(6)
+        bank_pass(6, 0, (0, 1), 1)
         L(4, 1, 0)
         L(5, 1, 0)
-        G(0, 0)
+        W(5)
+        W(4)
+        I("S", "za", 1, 1, 0)
+        L(5, 0, 0)
+        Z("za", 1, 1)
         W(6)
+        bank_pass(6, 0, (2, 3), 1)
+        bank_pass(6, 1, (0, 1), 0)
+        bank_pass(6, 1, (2, 3), 0)
+        L(5, 0, 1)
+        L(5, 1, 1)
+        goal_term(4)
+        E(5, 0)
+        C("S", 7, 1)
+        E(5, 1)
+        L(6, 1, 0)
         bank_pass(4, 0, (0, 1), 5)
         L(4, 1, 1)
-        store(3)
-        QM(6)
+        G(3, 0)
         C("S", 7, 0)
-        W(5)
-        bank_pass(5, 0, (0, 1), 7)
-        bank_pass(4, 0, (2, 3), 5)
-        G(5, 0)
-        W(4)
-        bank_pass(5, 0, (2, 3), 7)
-        L(5, 1, 1)
-        G(0, 1)
-        E(5, 1)
-        bank_pass(6, 0, (0, 1), 1)
-        L(5, 0, 0)
-        bank_pass(6, 1, (0, 1), 0)
-        L(5, 0, 1)
-        G(5, 1)
-        E(4, 1)
-        G(1, 1)
-        QM(7)
-        bank_pass(6, 0, (2, 3), 1)
-        bank_pass(6, 1, (2, 3), 0)
-        store(2)
-        L(6, 1, 0)
+        goal_term(5)
         L(6, 1, 1)
-        L(4, 0, 0)
-        L(4, 0, 1)
-        G(3, 1)
         L(6, 0, 0)
+        QM(7)
+        goal_term(6)
+        bank_pass(4, 0, (2, 3), 5)
+        L(4, 0, 0)
+        E(4, 1)
+        store(2)
+        G(5, 1)
+        L(4, 0, 1)
+        W(7)
+        E(4, 0)
+        store(3)
         bank_pass(7, 1, (0, 1), 2)
-        E(5, 0)
-        bank_pass(7, 1, (2, 3), 2)
-        G(6, 0)
-        G(4, 0)
-        store(0)
         E(6, 1)
-        L(6, 0, 1)
+        bank_pass(7, 1, (2, 3), 2)
         G(4, 1)
         L(7, 1, 0)
+        L(6, 0, 1)
         L(7, 1, 1)
         bank_pass(7, 0, (0, 1), 3)
-        G(6, 1)
-        E(4, 0)
         bank_pass(7, 0, (2, 3), 3)
-        store(5)
-        W(7)
         E(6, 0)
         E(7, 1)
+        store(5)
+        G(6, 1)
+        goal_term(7)
         L(7, 0, 0)
         store(4)
-        G(7, 1)
         L(7, 0, 1)
+        E(7, 0)
+        G(7, 1)
         store(6)
         store(7, 1)
-        E(7, 0)
         store(7, 0)
-        G(7, 0)

from contextlib import ExitStack

import concourse.mybir as mybir
from concourse.masks import make_identity

F32 = mybir.dt.float32
BF16 = mybir.dt.bfloat16
U32 = mybir.dt.uint32
I32 = mybir.dt.int32
U8 = mybir.dt.uint8
FP8X4 = mybir.dt.float8_e4m3fn_x4
FP4X4 = mybir.dt.float4_e2m1fn_x4
MULT = mybir.AluOpType.mult
SUB = mybir.AluOpType.subtract

D, B, Q = 1024, 1024, 2048
P = 128
N = 512
KP = 512
FLOPS = 2 * D * D * (B + Q)
V_COLS = 256


def tile_barlow_twins_bank_s1_kernel(tc, za, zb, ma, mb_words, mb_scales, ra, rb, goal, pair, out):
    nc = tc.nc
    with ExitStack() as ctx:
        keep = ctx.enter_context(tc.tile_pool(name="keep", bufs=1))
        stage = ctx.enter_context(tc.tile_pool(name="stage", bufs=4))
        psum = ctx.enter_context(tc.psum_pool(name="psum", bufs=1))
        ctx.enter_context(tc.manual_schedule())

        ident = keep.tile([P, P], F32, name="ident", align_bytes=64)
        ident_bf = keep.tile([P, P], BF16, name="ident_bf", align_bytes=64)
        vec = keep.tile([P, P], BF16, name="vec", align_bytes=64)
        cols = keep.tile([P, 24], F32, name="cols", align_bytes=64)
        rb_col = keep.tile([P, 8], BF16, name="rb_col", align_bytes=64)
        rb_all = keep.tile([P, D], BF16, name="rb_all", align_bytes=64)
        mbw = keep.tile([P, 4, 2 * D], U8, name="mbw", align_bytes=256)
        mbs = keep.tile([P, 4, D], U8, name="mbs", align_bytes=256)
        za_codes = keep.tile([P, 2, D], U32, name="za_codes", align_bytes=256)
        za_scales = keep.tile([P, 2, D], U8, name="za_scales", align_bytes=256)
        zb_codes = keep.tile([P, 2, D], U32, name="zb_codes", align_bytes=256)
        zb_scales = keep.tile([P, 2, D], U8, name="zb_scales", align_bytes=256)
        ma_codes = [keep.tile([P, 4, P], U32, name="ma_codes%d" % i, align_bytes=256) for i in range(8)]
        ma_scales = [keep.tile([P, 4, P], U8, name="ma_scales%d" % i, align_bytes=256) for i in range(8)]
        ma_raw = [keep.tile([P, Q], BF16, name="ma_raw%d" % i, align_bytes=64) for i in range(8)]
        zb_raw = [keep.tile([P, 4, D], BF16, name="zb_raw%d" % g, align_bytes=64) for g in range(2)]
        za_raw = [[keep.tile([P, 4, N], BF16, name="za_raw%d%d" % (g, h), align_bytes=64) for h in range(2)] for g in range(2)]
        pair_sb = [keep.tile([P, 2, D], BF16, name="pair%d" % i, align_bytes=64) for i in range(4)]

        za_v = za.rearrange("(g p j) w -> g p j w", p=P, j=4)
        zb_v = zb.rearrange("(g p j) w -> g p j w", p=P, j=4)
        pair_v = pair.rearrange("(a i p) n -> a p i n", i=2, p=P)
        mbw_v = mb_words.bitcast(I32).rearrange("g p b -> p g b")

        def load_ma(i, k0=0, k1=Q):
            nc.sync.dma_start(out=ma_raw[i][:, k0:k1], in_=ma[P * i : P * (i + 1), k0:k1])

        def load_mb(a):
            nc.sync.dma_start(out=mbw[:, 2 * a : 2 * a + 2, :].bitcast(I32), in_=mbw_v[:, 2 * a : 2 * a + 2, :])

        def load_zb(g):
            nc.sync.dma_start(out=zb_raw[g][:], in_=zb_v[g])

        def load_za(g, h):
            nc.sync.dma_start(out=za_raw[g][h][:], in_=za_v[g][:, :, N * h : N * (h + 1)])

        def load_pair(a):
            nc.sync.dma_start(out=pair_sb[a][:], in_=pair_v[a])

        nc.gpsimd.memset(vec[:], 0.0)
        nc.vector.memset(mbs[:].rearrange("p g n -> p (g n)").bitcast(I32), 0)
        make_identity(nc, ident[:])
        nc.vector.tensor_copy(out=ident_bf[:], in_=ident[:])

        def load_vectors():
            for v, src in enumerate((ra, rb, goal)):
                nc.sync.dma_start(out=vec[8 * v : 8 * v + 8, :], in_=src.rearrange("(c p) -> c p", p=P))

        def load_scales():
            for q in range(4):
                nc.sync.dma_start(
                    out=mbs[32 * q : 32 * q + 4, :, :].bitcast(I32),
                    in_=mb_scales[:, 4 * q : 4 * q + 4, :].bitcast(I32).rearrange("g r n -> r g n"),
                )

        turned = {}
        small = {}
        grouped = {}
        zgrouped = {}
        acc = {}
        result = {}

        sorted_words = {}

        def X(eng, i):
            w = stage.tile([P, 4, 2, P], F32, name="words%d" % i, tag="words", align_bytes=64)
            sorted_words[i] = w
            src = ma_raw[i][:].bitcast(F32).rearrange("p (g m u) -> p g u m", g=4, u=2)
            if eng == "S":
                nc.scalar.copy(out=w[:], in_=src)
            else:
                nc.vector.tensor_copy(out=w[:], in_=src)

        def T(i, b, bank):
            t = psum.tile([P, 2, 2, P], F32, name="turned%d_%d" % (i, b), tag="bank%d" % bank)
            turned[i, b] = t
            words = ma_raw[i][:].bitcast(F32)
            for gg in range(2):
                g = 2 * b + gg
                for u in range(2):
                    if i in sorted_words:
                        src = sorted_words[i][:, g, u, :]
                    else:
                        src = words[:, 256 * g + u : 256 * (g + 1) : 2]
                    nc.tensor.transpose(t[:, gg, u, :], src, ident[:])

        def C(eng, i, b):
            if i not in grouped:
                grouped[i] = stage.tile([P, 4, P, 4], BF16, name="ma_grouped%d" % i, tag="ma_grouped", align_bytes=64)
            dst = grouped[i][:, 2 * b : 2 * b + 2, :, :].rearrange("p g m t -> p (g m t)").bitcast(F32)
            dst = dst.rearrange("p (g m u) -> p g m u", g=2, u=2)
            src = turned[i, b][:].rearrange("p g u m -> p g m u")
            if eng == "S":
                nc.scalar.copy(out=dst, in_=src)
            else:
                nc.vector.tensor_copy(out=dst, in_=src)

        def QM(i, g0=0, g1=4):
            nc.vector.quantize_mx(
                out=ma_codes[i][:, g0:g1, :].rearrange("p g m -> p (g m)").bitcast(FP8X4),
                scales=ma_scales[i][:, g0:g1, :].rearrange("p g m -> p (g m)"),
                in_=grouped[i][:, g0:g1, :, :].rearrange("p g m t -> p (g m t)"),
            )

        def I(eng, z, g, h, v_cols=V_COLS):
            if (z, g, h) not in zgrouped:
                zgrouped[z, g, h] = stage.tile([P, N, 4], BF16, name="%s_grouped%d%d" % (z, g, h), tag="z_grouped", align_bytes=64)
            dst = zgrouped[z, g, h]
            src = zb_raw[g][:, :, N * h : N * (h + 1)] if z == "zb" else za_raw[g][h][:]
            if eng == "V":
                nc.vector.tensor_copy(
                    out=dst[:, 0:v_cols, :].rearrange("p (c i) j -> p c j i", i=4),
                    in_=src[:, :, 0:v_cols].rearrange("p j (c i) -> p c j i", i=4),
                )
            else:
                nc.scalar.copy(
                    out=dst[:, v_cols:N, :].rearrange("p (c i) j -> p c j i", i=4),
                    in_=src[:, :, v_cols:N].rearrange("p j (c i) -> p c j i", i=4),
                )

        def Z(z, g, h):
            codes, scales = (zb_codes, zb_scales) if z == "zb" else (za_codes, za_scales)
            nc.vector.quantize_mx(
                out=codes[:, g, N * h : N * (h + 1)].bitcast(FP8X4),
                scales=scales[:, g, N * h : N * (h + 1)],
                in_=zgrouped[z, g, h][:].rearrange("p w j -> p (w j)"),
            )

        def bank_pass(i, h, gs, bank):
            if (i, h) not in acc:
                acc[i, h] = psum.tile([P, N], F32, name="acc%d_%d" % (i, h), tag="bank%d" % bank)
            for g in gs:
                nc.tensor.matmul_mx(
                    out=acc[i, h][:],
                    lhsT=ma_codes[i][:, g, :].bitcast(FP8X4),
                    lhsT_scale=ma_scales[i][:, g, :],
                    rhs=mbw[:, g, 2 * N * h : 2 * N * (h + 1)].bitcast(FP4X4),
                    rhs_scale=mbs[:, g, N * h : N * (h + 1)],
                    start=(g == 0),
                    stop=False,
                )

        def TT(i, bank):
            T(i, 0, bank)
            T(i, 1, bank + 1)

        def B(i, h, bank):
            bank_pass(i, h, (0, 1, 2, 3), bank)

        def L(i, h, g):
            nc.tensor.matmul_mx(
                out=acc[i, h][:],
                lhsT=za_codes[:, g, P * i : P * (i + 1)].bitcast(FP8X4),
                lhsT_scale=za_scales[:, g, P * i : P * (i + 1)],
                rhs=zb_codes[:, g, N * h : N * (h + 1)].bitcast(FP8X4),
                rhs_scale=zb_scales[:, g, N * h : N * (h + 1)],
                start=False,
                stop=(g == 1),
            )

        def E(i, h):
            if i not in result:
                result[i] = stage.tile([P, D], F32, name="result%d" % i, tag="result", bufs=5, align_bytes=64)
            c = slice(N * h, N * (h + 1))
            nc.vector.scalar_tensor_tensor(
                out=result[i][:, c], in0=acc[i, h][:], scalar=cols[:, i : i + 1], in1=weight[i][:, c], op0=MULT, op1=MULT
            )

        def G(i, h):
            if h == i // 4:
                blk = result[i][:, P * i : P * (i + 1)]
                nc.gpsimd.tensor_tensor(out=blk, in0=blk, in1=diag[i][:], op=SUB)

        weight = {}
        diag = {}

        def W(i):
            weight[i] = stage.tile([P, D], F32, name="weight%d" % i, tag="weight", bufs=4, align_bytes=64)
            src = pair_sb[i // 2][:, i % 2, :]
            nc.vector.tensor_tensor(out=weight[i][:], in0=src, in1=rb_all[:], op=MULT)

        def goal_term(i):
            diag[i] = stage.tile([P, P], F32, name="diag%d" % i, tag="diag", bufs=4, align_bytes=64)
            src = pair_sb[i // 2][:, i % 2, P * i : P * (i + 1)]
            nc.scalar.activation(out=diag[i][:], in_=src, func=mybir.ActivationFunctionType.Copy, scale=cols[:, 16 + i : 17 + i])
            nc.gpsimd.tensor_tensor(out=diag[i][:], in0=diag[i][:], in1=ident[:], op=MULT)

        def store(i, h=None):
            c = slice(0, D) if h is None else slice(N * h, N * (h + 1))
            nc.sync.dma_start(out=out[P * i : P * (i + 1), c], in_=result[i][:, c])

        def vec_turn():
            small["vec"] = psum.tile([P, P], BF16, name="vec_t", tag="bank4")
            nc.tensor.transpose(small["vec"][:], vec[:], ident_bf[:])

        def vec_take():
            nc.vector.tensor_copy(out=rb_col[:], in_=small["vec"][:, 8:16])
            nc.vector.tensor_copy(out=cols[:], in_=small["vec"][:, 0:24])

        def rb_turn():
            small["rb"] = psum.tile([P, D], BF16, name="rb_t", tag="bank7")
            for c in range(8):
                nc.tensor.transpose(small["rb"][:, P * c : P * (c + 1)], rb_col[:, c : c + 1].to_broadcast([P, P]), ident_bf[:])

        def rb_take():
            nc.scalar.copy(out=rb_all[:], in_=small["rb"][:])

        load_ma(0, 0, D)
        load_vectors()
        vec_turn()
        load_ma(0, D, Q)
        T(0, 0, 0)
        vec_take()
        T(0, 1, 1)
        C("V", 0, 0)
        load_ma(2)
        T(2, 1, 5)
        C("S", 0, 1)
        load_zb(0)
        load_ma(1)
        T(2, 0, 4)
        rb_turn()
        load_mb(0)
        C("V", 2, 1)
        C("S", 2, 0)
        I("S", "zb", 0, 0, 256)
        QM(0)
        QM(2)
        load_scales()
        rb_take()
        T(1, 0, 2)
        I("V", "zb", 0, 0, 256)
        I("V", "zb", 0, 1, 384)
        load_ma(3)
        load_za(0, 0)
        Z("zb", 0, 0)
        T(1, 1, 3)
        bank_pass(0, 1, (0, 1), 1)
        C("S", 1, 1)
        I("S", "zb", 0, 1, 384)
        T(3, 0, 6)
        T(3, 1, 7)
        load_zb(1)
        load_mb(1)
        C("V", 1, 0)
        load_za(1, 0)
        C("S", 3, 0)
        load_pair(0)
        QM(1)
        Z("zb", 0, 1)
        bank_pass(0, 0, (0, 1), 0)
        bank_pass(2, 0, (0, 1), 4)
        bank_pass(1, 0, (0, 1), 2)
        I("V", "za", 0, 0, 384)
        C("S", 3, 1)
        load_ma(4)
        I("S", "za", 0, 0, 384)
        bank_pass(2, 1, (0, 1), 5)
        QM(3)
        Z("za", 0, 0)
        I("V", "zb", 1, 1, 256)
        I("S", "zb", 1, 0, 320)
        bank_pass(3, 1, (0, 1), 7)
        I("V", "zb", 1, 0, 320)
        load_ma(5)
        bank_pass(3, 0, (0, 1), 6)
        load_za(0, 1)
        bank_pass(1, 1, (0, 1), 3)
        load_pair(1)
        Z("zb", 1, 0)
        bank_pass(1, 1, (2, 3), 3)
        L(1, 1, 0)
        bank_pass(0, 0, (2, 3), 0)
        I("S", "zb", 1, 1, 256)
        I("V", "za", 1, 0, 128)
        bank_pass(2, 1, (2, 3), 5)
        bank_pass(0, 1, (2, 3), 1)
        bank_pass(1, 0, (2, 3), 2)
        L(1, 0, 0)
        Z("zb", 1, 1)
        W(1)
        bank_pass(2, 0, (2, 3), 4)
        I("S", "za", 1, 0, 128)
        L(0, 1, 0)
        Z("za", 1, 0)
        L(0, 0, 0)
        L(1, 0, 1)
        L(0, 0, 1)
        W(0)
        load_ma(6)
        E(1, 0)
        L(1, 1, 1)
        bank_pass(3, 1, (2, 3), 7)
        L(0, 1, 1)
        E(0, 0)
        goal_term(1)
        E(0, 1)
        bank_pass(3, 0, (2, 3), 6)
        E(1, 1)
        W(2)
        X("S", 4)
        load_ma(7)
        L(2, 0, 0)
        goal_term(0)
        X("V", 6)
        X("S", 5)
        I("S", "za", 0, 1, 0)
        L(2, 0, 1)
        G(0, 0)
        T(4, 1, 1)
        load_za(1, 1)
        T(4, 0, 0)
        T(5, 1, 3)
        C("S", 4, 0)
        C("S", 4, 1)
        load_pair(2)
        E(2, 0)
        T(5, 0, 2)
        L(2, 1, 0)
        L(3, 1, 0)
        load_pair(3)
        L(3, 1, 1)
        QM(4)
        L(3, 0, 0)
        C("S", 5, 1)
        W(3)
        L(3, 0, 1)
        G(1, 0)
        T(6, 0, 0)
        L(2, 1, 1)
        bank_pass(4, 1, (0, 1), 4)
        C("S", 5, 0)
        QM(5)
        bank_pass(4, 1, (2, 3), 4)
        X("S", 7)
        store(1)
        goal_term(2)
        T(6, 1, 1)
        store(0)
        T(7, 1, 3)
        T(7, 0, 2)
        E(3, 0)
        E(2, 1)
        E(3, 1)
        G(2, 0)
        goal_term(3)
        C("S", 6, 1)
        bank_pass(5, 1, (0, 1), 6)
        bank_pass(5, 1, (2, 3), 6)
        bank_pass(5, 0, (0, 1), 7)
        bank_pass(5, 0, (2, 3), 7)
        Z("za", 0, 1)
        C("S", 6, 0)
        QM(6)
        bank_pass(6, 0, (0, 1), 1)
        L(4, 1, 0)
        L(5, 1, 0)
        W(5)
        W(4)
        I("S", "za", 1, 1, 0)
        L(5, 0, 0)
        Z("za", 1, 1)
        W(6)
        bank_pass(6, 0, (2, 3), 1)
        bank_pass(6, 1, (0, 1), 0)
        bank_pass(6, 1, (2, 3), 0)
        L(5, 0, 1)
        L(5, 1, 1)
        goal_term(4)
        E(5, 0)
        C("S", 7, 1)
        E(5, 1)
        L(6, 1, 0)
        bank_pass(4, 0, (0, 1), 5)
        L(4, 1, 1)
        G(3, 0)
        C("S", 7, 0)
        goal_term(5)
        L(6, 1, 1)
        L(6, 0, 0)
        QM(7)
        goal_term(6)
        bank_pass(4, 0, (2, 3), 5)
        L(4, 0, 0)
        E(4, 1)
        store(2)
        G(5, 1)
        L(4, 0, 1)
        W(7)
        E(4, 0)
        store(3)
        bank_pass(7, 1, (0, 1), 2)
        E(6, 1)
        bank_pass(7, 1, (2, 3), 2)
        G(4, 1)
        L(7, 1, 0)
        L(6, 0, 1)
        L(7, 1, 1)
        bank_pass(7, 0, (0, 1), 3)
        bank_pass(7, 0, (2, 3), 3)
        E(6, 0)
        E(7, 1)
        store(5)
        G(6, 1)
        goal_term(7)
        L(7, 0, 0)
        store(4)
        L(7, 0, 1)
        E(7, 0)
        G(7, 1)
        store(6)
        store(7, 1)
        store(7, 0)
